import numpy as np, ml_dtypes
CORES = [40,64,80,88,96,104,120,144]
N = 8
BF = ml_dtypes.bfloat16
def gentries(a):
    return np.ascontiguousarray(a.reshape(8, 16, -1).transpose(0, 2, 1)).reshape(8, -1)
def gtable(e):
    e = np.asarray(e); return np.ascontiguousarray(e.reshape(8, -1, 16).transpose(0, 2, 1)).reshape(128, -1).astype(np.int32)
P, M, W, CAP, S, RO = 1792, 1536, 3328, 768, 3, 3
def parts(rng):
    x = rng.integers(0, 16, (N, 8, 16, W), dtype=np.int16)
    src = rng.integers(0, W, (N, 8, M)); trig = rng.integers(0, W, (N, 8, M))
    tg = np.ascontiguousarray(np.argsort(rng.random((N, 8, W)), axis=-1)[..., :M])
    th = rng.choice(np.array([66, 74, 80, 86, 92]), (N, 8, 1)); th[0, 0] = 66; th[1, 1] = 92
    return x, src, trig, tg, th
def dist(x, trig):
    return np.add.reduce(np.abs(np.take_along_axis(x, trig[:, :, None, :], 3) - x[..., P:]), axis=2)
def aim(rng, x, th, want):
    none = np.zeros((N, 8, M), np.int64)
    t = np.where(want, P + np.arange(M), np.where(dist(x, none) >= dist(x, none + 1), 0, 1))
    for k in range(4):
        c = rng.integers(0, W, (N, 8, M)); t = np.where((dist(x, c) < th) == want, c, t)
    return t
def aimed(rng, e, b):
    o = rng.permutation(W); t = o[~np.isin(o, b)][:M]; t[e] = b
    return t
def apart(rng, n):
    return np.stack([2 * rng.permutation(M // 2)[:n] + rng.integers(0, 2, n) for r in range(N)])
def pack(x, src, trig, tg, th):
    return {"x": x.reshape(N, 128, W).astype(np.float32).astype(BF), "src": np.stack([gtable(a) for a in src]), "trig": np.stack([gtable(a) for a in trig]),
            "tg": np.stack([gtable(a) for a in tg]), "th": np.ascontiguousarray(np.repeat(th, 16, axis=2).reshape(N, 128, 1)).astype(np.int32)}
def setup_inputs(rng):
    return pack(*parts(rng))
def setup_inputs_room(rng):
    x, src, trig, tg, th = parts(rng); x[..., 0] = 0; x[..., 1] = 15
    n = rng.choice(np.array([0, 1, CAP - 1, CAP, CAP + 1, M]), (N, 8)); n[0] = np.array([CAP, CAP + 1, M, CAP - 1, 1, 0, CAP, CAP + 1])
    n[1] = rng.permutation(np.arange(2, 10)); n[2] = rng.permutation(np.arange(10, 18))
    key = rng.random((N, 8, M)); key[0, :, M - 1] = -1.0
    want = np.argsort(np.argsort(key, axis=-1), axis=-1) < n[:, :, None]
    return pack(x, src, aim(rng, x, th, want), tg, th)
def setup_inputs_ties(rng):
    x, src, trig, tg, th = parts(rng)
    lo = rng.choice(np.array([0, 4, 7]), (N, 8, 1, 1)); lo[0, :3] = np.array([0, 4, 7]).reshape(3, 1, 1); lo[1:, 3] = 0; lo[:, 4] = 7
    x = lo + (15 - 2 * lo) * rng.integers(0, 2, (N, 8, 16, W))
    th = 8 * (15 - 2 * lo[..., 0]) + rng.integers(0, 2, (N, 8, 1)); th[0, 3] = 0; th[1, 3] = 241; th[2, 3] = 240; th[3:, 3] = rng.integers(161, 241, (N - 3, 1))
    x[1:, 3, :, 0] = 0; x[1:, 3, :, P:P + 8] = 15; trig[1:, 3, :8] = 0
    th[:, 4] = 1 + (np.arange(N)[:, None] + rng.integers(0, 7)) % 7
    m = x[:, 4, :, P:P + 8]; x[:, 4, :, :8] = np.where(np.arange(16)[:, None] < np.arange(8), 15 - m, m); trig[:, 4, :8] = np.arange(8)
    return pack(x, src, trig, tg, th)
def setup_inputs_alike(rng):
    x, src, trig, tg, th = parts(rng); e = np.arange(M); h = min(P, M - M // 16); low = e % 16 < 8
    for q in range(N):
        tg[q, 0] = P + rng.permutation(M)
        tg[q, 1] = rng.permutation(np.concatenate([rng.permutation(P)[:h], P + rng.permutation(M)[:M - h]]))
        tg[q, 2] = P + (2 * rng.permutation(M // 2)[:, None] + np.array([0, 1])).reshape(-1)
        tg[q, 3, low] = P + 2 * rng.permutation(M // 2); tg[q, 3, ~low] = rng.permutation(P)[:M // 2]
        o = rng.permutation(W); tg[q, 5] = o[np.argsort((o + rng.integers(0, 16)) % 16, kind="stable")][:M]
        tg[q, 7] = e if q % 2 == 0 else W - 1 - e
    x[:, 2, :, P + 1::2] = x[:, 2, :, P::2]; trig[:, 2, 1::2] = trig[:, 2, ::2]
    src[:, 3] = rng.integers(0, P, (N, M)); trig[:, 3] = np.where(low, P + e, rng.integers(0, P, (N, M))); th[:, 3] = 1
    x[:, 4, :, P:] = rng.integers(0, 8, (N, 16, M)); x[:, 5, :, P:] = rng.integers(8, 16, (N, 16, M)); th[:, 5] = 241
    src[:, 6] = rng.choice(np.array([0, W - 1, P - 1, P]), (N, M)); trig[:, 6] = rng.choice(np.array([0, W - 1, P - 1, P]), (N, M))
    trig[:, 7] = P + e; th[:, 7] = 1
    return pack(x, src, trig, tg, th)
def setup_inputs_cold(rng):
    x, src, trig, tg, th = parts(rng); q = rng.permutation(N); g = rng.permutation(8)
    th[q[0]] = 0; th[q[1]] = 241
    th[:, g[:3]] = 0; th[3, g[1]] = 80; th[rng.integers(0, N), g[2]] = 80
    for k in g[3:6]:
        th[:, k] = 1; src[:, k] = rng.integers(0, P, (N, M)); trig[:, k] = rng.integers(0, P, (N, M))
    for k, n in ((g[3], 5), (g[4], int(rng.integers(2, 18)))):
        e = np.sort(apart(rng, n), axis=1)
        for r in range(N):
            trig[r, k, e[r]] = P + e[r]; tg[r, k] = aimed(rng, e[r], P + np.roll(e[(r + S) % N], -1))
    k = g[5]; n = int(rng.integers(2, 18)); e = apart(rng, 2 * n); a = e[:, :n]; b = e[:, n:]
    for r in range(N):
        s = (r + S) % N
        x[r, k][:, P + a[r]] = rng.integers(0, 8, (16, n)); trig[r, k, a[r]] = P + a[r]; src[r, k, b[r]] = P + b[r]
        tg[r, k] = aimed(rng, np.concatenate([a[r], b[r] ^ 1]), P + np.concatenate([b[s], a[s]]))
    return pack(x, src, trig, tg, th)
def setup_inputs_spread(rng):
    x, src, trig, tg, th = parts(rng)
    level = rng.integers(0, 16, (N, 8, 1, W)).astype(np.float32); width = np.exp2(rng.integers(-1, 4, (N, 8, 1, W))).astype(np.float32)
    x = np.clip(np.rint(level + width * rng.standard_normal((N, 8, 16, W), dtype=np.float32)), 0, 15).astype(np.int16)
    src = np.minimum((W * rng.random((N, 8, M)) ** 3).astype(np.int64), W - 1); trig = np.minimum((W * rng.random((N, 8, M)) ** 2).astype(np.int64), W - 1)
    tg[:, 1::2] = np.sort(tg[:, 1::2], axis=-1); th = rng.integers(20, 161, (N, 8, 1))
    return pack(x, src, trig, tg, th)
def check_inputs(d):
    bad = []
    v = np.asarray(d["x"], np.float32)
    if not (np.min(v) >= 0 and np.max(v) <= 15 and np.all(v == np.floor(v))): bad.append("numbers of x")
    for k, lo, hi in (("src", 0, W - 1), ("trig", 0, W - 1), ("tg", 0, W - 1), ("th", 0, 241)):
        if np.min(d[k]) < lo or np.max(d[k]) > hi: bad.append("range of " + k)
    o = np.sort(np.stack([gentries(a) for a in d["tg"]]), axis=-1)
    if np.any(o[..., 1:] == o[..., :-1]): bad.append("targets of a rank and group differ")
    t = np.asarray(d["th"]).reshape(N, 8, 16)
    if np.any(t != t[:, :, :1]): bad.append("rows of th alike in a group")
    return bad
def reference(x, src, trig, tg, th):
    v = x.astype(np.float32).astype(np.int32).reshape(N, 8, 16, W); lim = th.astype(np.int64).reshape(N, 8, 16)[:, :, :1]
    so = np.stack([gentries(a) for a in src]).astype(np.int64); tr = np.stack([gentries(a) for a in trig]).astype(np.int64); ta = np.stack([gentries(a) for a in tg]).astype(np.int64)
    mate = np.arange(M) ^ 1
    for rnd in range(RO):
        m = v[..., P:]
        far = np.add.reduce(np.abs(np.take_along_axis(v, tr[:, :, None, :], 3) - m), axis=2)
        c = (far < lim).astype(np.int64); go = (c == 1) & (np.add.accumulate(c, axis=2) <= CAP)
        a = np.where(m >= 8, 15 - np.take_along_axis(v, so[:, :, None, :], 3), -1)
        nv = v + 0; ns = so + 0; nt = tr + 0; ng = ta + 0
        for q in range(N):
            r = (q + S) % N
            for g in range(8):
                i = np.flatnonzero(go[q, g]); b = ta[q, g, i]; col = a[q, g][:, i]
                nv[r, g][:, b] = np.where(col >= 0, col, v[r, g][:, b])
                j = b >= P; e = b[j] - P
                nt[r, g, e] = so[r, g, e]; ns[r, g, e] = so[q, g, i[j]]
                hit = np.zeros(M, bool); hit[e] = True
                ng[r, g] = np.where(hit != hit[mate], ta[r, g][mate], ta[r, g])
        v, so, tr, ta = nv, ns, nt, ng
    return {"yx": v.reshape(N, 128, W).astype(np.float32).astype(BF), "ysrc": np.stack([gtable(a) for a in so]).astype(np.float32),
            "ytrig": np.stack([gtable(a) for a in tr]).astype(np.float32), "ytg": np.stack([gtable(a) for a in ta]).astype(np.float32)}

@@ -1,0 +1,374 @@
+from concourse.mybir import AluOpType as A, ActivationFunctionType as F
+
+N, P, M, W, CAP, STEP, RO = 8, 1792, 1536, 3328, 768, 3, 3
+KC = M // 16
+BIG = 4096.0
+TH = float(CAP - 2048)
+DCH = [(72, 96, "s", "pT2"), (0, 32, "v", "pT0"), (32, 56, "v", "pT1"), (56, 72, "v", "pZ")]
+MCH = [(0, 32), (32, 64), (64, 96)]
+SCH = [(0, 24), (24, 48), (48, 72), (72, 96)]
+
+SCRATCH = {
+    "V": ("sbuf", [128, 2 * W], "bfloat16"), "B": ("sbuf", [128, M], "bfloat16"),
+    "D": ("sbuf", [128, M], "bfloat16"), "K": ("sbuf", [128, M], "bfloat16"), "Y": ("sbuf", [128, M], "bfloat16"),
+    "Tt": ("sbuf", [128, M], "bfloat16"), "GS": ("sbuf", [128, M], "bfloat16"), "SW": ("sbuf", [128, M + 16], "bfloat16"),
+    "wA": ("sbuf", [128, W], "float32"), "wB": ("sbuf", [128, W], "float32"), "val": ("sbuf", [128, M // 2], "float32"),
+    "zA": ("sbuf", [128, 208], "float32"), "zB": ("sbuf", [128, 208], "float32"),
+    "uA": ("sbuf", [128, 16, 13], "float32"), "uB": ("sbuf", [128, 16, 13], "float32"),
+    "i1": ("sbuf", [128, 16, 6], "float32"), "i2": ("sbuf", [128, 16, 6], "float32"), "i3": ("sbuf", [128, 16, 6], "int32"),
+    "invS": ("sbuf", [128, KC], "uint16"), "invL": ("sbuf", [128, KC], "uint16"),
+    "tgi": ("sbuf", [128, KC], "int32"), "tri": ("sbuf", [128, KC], "int32"), "sri": ("sbuf", [128, KC], "int32"),
+    "thi": ("sbuf", [128, 1], "int32"), "thf": ("sbuf", [128, 1], "float32"),
+    "ci": ("sbuf", [128, KC], "int32"), "tpu": ("sbuf", [128, KC], "uint16"),
+    "tru": ("sbuf", [128, KC], "uint16"), "sru": ("sbuf", [128, KC], "uint16"),
+    "G2": ("sbuf", [128, 2 * KC], "bfloat16"), "thr": ("sbuf", [128, 2 * KC], "float32"),
+    "J": ("sbuf", [128, 144], "float32"), "GB": ("sbuf", [128, 128], "float32"),
+    "pi": ("sbuf", [128, 1], "int32"), "gbi": ("sbuf", [128, 1], "int32"),
+    "E": ("sbuf", [128, 144], "bfloat16"), "E2": ("sbuf", [128, 144], "bfloat16"),
+    "If": ("sbuf", [128, 128], "float32"), "SI": ("sbuf", [128, 128], "float32"),
+}
+for _n in ("pf", "gbf", "w1", "w2"):
+    SCRATCH[_n] = ("sbuf", [128, 1], "float32")
+for _n in ("nJ", "I", "Sw", "nI", "OB", "nOB", "Ua", "U", "Ub", "Um"):
+    SCRATCH[_n] = ("sbuf", [128, 128], "bfloat16")
+for _n in ("trf", "srf", "tgf", "d1", "f1", "f2", "f3", "f4", "f5", "Af", "x1"):
+    SCRATCH[_n] = ("sbuf", [128, KC], "float32")
+for _n in ("cb", "Pb", "hit", "pb"):
+    SCRATCH[_n] = ("sbuf", [128, KC], "bfloat16")
+for _n in ("pT0", "pT1", "pT2", "pF", "pZ", "pH", "pM", "pC"):
+    SCRATCH[_n] = ("psum", [128, 512], "float32")
+SEMAPHORES = ["sv", "ss", "sp", "sg", "ltg", "lx", "ltr", "lsr", "lth", "iA", "iB", "oA", "oB", "ox", "ol", "sent", "aI"]
+for _r in range(RO):
+    for _s in "SL":
+        SCRATCH["m%s%d" % (_s, _r)] = ("sbuf", [128, M], "bfloat16")
+        SCRATCH["E%s%d" % (_s, _r)] = ("sbuf", [128, KC], "uint16")
+        SCRATCH["G%s%d" % (_s, _r)] = ("sbuf", [128, KC], "uint16")
+        SCRATCH["O%s%d" % (_s, _r)] = ("sbuf", [128, 3 * KC], "bfloat16")
+    SEMAPHORES += ["aE%d" % _r, "aG%d" % _r, "aO%d" % _r, "fl%d" % _r] + ["am%d_%d" % (_r, _c) for _c in range(3)]
+
+
+def helpers(T, topo, q):
+    a, b = T.cores[q], T.cores[(q + STEP) % N]
+    if topo.may_write(a, b):
+        return None
+    c = [k for k in topo.cores_of(a) if topo.may_write(k, b) and T.rank_of(k) is None]
+    c.sort(key=lambda k: topo.die(k) != topo.die(a))
+    return c[0], c[1]
+
+
+def landing(T, kind, r, c):
+    if kind == "I":
+        return T.invL[:], "aI"
+    if kind == "m":
+        return T["mL%d" % r][:, 16 * MCH[c][0]:16 * MCH[c][1]], "am%d_%d" % (r, c)
+    return T["%sL%d" % (kind, r)][:], "a%s%d" % (kind, r)
+
+
+def write(g, T, topo, me, to, out, in_, sem):
+    rid, pid = topo.addr(to, me)
+    g.remote_dma(out, in_, T.sem[sem], T.sem.sent, pid, rid, topo.mask(me, to))
+    return len(topo.engines(me, to))
+
+
+def hand_on(g, core, T, topo, q, lists):
+    a, b = T.cores[q], T.cores[(q + STEP) % N]
+    n, sent = len(topo.engines(a, core)), 0
+    for r in range(RO):
+        order = [("E", 0), ("G", 0), ("O", 0)] + ([("I", 0)] if r == 0 else []) if lists else [("m", c) for c in range(3)]
+        for kind, c in order:
+            ap, sem = landing(T, kind, r, c)
+            g.wait_ge(T.sem[sem], n)
+            sent += write(g, T, topo, core, b, ap, ap, sem)
+    g.wait_ge(T.sem.sent, sent)
+
+
+def rank_program(g, core, T, topo):
+    rank = T.rank_of(core)
+    if rank is None:
+        for q in range(N):
+            h = helpers(T, topo, q)
+            if h is not None and core in h:
+                hand_on(g, core, T, topo, q, core == h[0])
+        return
+
+    nxt, prv = T.cores[(rank + STEP) % N], (rank - STEP) % N
+    h_out, h_in = helpers(T, topo, rank), helpers(T, topo, prv)
+    Q = {"v": g.vector, "s": g.scalar, "p": g.tensor, "g": g, "y": g.sync}
+    V, S, PE = g.vector, g.scalar, g.tensor
+    total, seen, lastw, readers = {}, {q: {} for q in Q}, {}, {}
+
+    def need(q, evs):
+        for name, val, snap in sorted(evs, key=lambda e: -len(e[2])):
+            if q == "p" and name == "sp":
+                continue
+            if seen[q].get(name, 0) < val:
+                Q[q].wait_ge(T.sem[name], val)
+                seen[q][name] = val
+                for k, v in snap.items():
+                    if seen[q].get(k, 0) < v:
+                        seen[q][k] = v
+
+    def before(q, rd, wr):
+        evs = [lastw[k] for k in rd + wr if k in lastw]
+        for k in wr:
+            evs += readers.get(k, [])
+        best = {}
+        for e in evs:
+            if e[0] not in best or best[e[0]][1] < e[1]:
+                best[e[0]] = e
+        need(q, list(best.values()))
+
+    def after(ev, rd, wr):
+        for k in rd:
+            readers.setdefault(k, []).append(ev)
+        for k in wr:
+            lastw[k] = ev
+            readers[k] = []
+
+    def op(q, rd, wr, *fns):
+        rd, wr = rd.split(), wr.split()
+        before(q, rd, wr)
+        for fn in fns:
+            ins = fn()
+        name = "s" + q
+        ins.then_inc(T.sem[name], 1)
+        total[name] = total.get(name, 0) + 1
+        after((name, total[name], dict(seen[q])), rd, wr)
+
+    def dma(q, name, rd, wr, *pairs):
+        rd, wr = rd.split(), wr.split()
+        before(q, rd, wr)
+        for out, in_ in pairs:
+            Q[q].dma_start(out, in_).then_inc(T.sem[name], 16)
+            total[name] = total.get(name, 0) + 16
+        after((name, total[name], dict(seen[q])), rd, wr)
+
+    def send(kind, r, c, rd, in_):
+        before("g", rd.split(), [])
+        ap, sem = landing(T, kind, r, c)
+        to = nxt if h_out is None else h_out[1 if kind == "m" else 0]
+        total["sent"] = total.get("sent", 0) + write(g, T, topo, core, to, ap, in_, sem)
+        frm = T.cores[prv] if h_in is None else h_in[1 if kind == "m" else 0]
+        total[sem] = len(topo.engines(frm, core))
+        lastw[sem] = (sem, total[sem], {})
+
+    def ts(rd, wr, out, in0, s1, op0, s2=None, op1=None):
+        if op1 is None:
+            op("v", rd, wr, lambda: V.tensor_scalar(out, in0, s1, None, op0))
+        else:
+            op("v", rd, wr, lambda: V.tensor_scalar(out, in0, s1, s2, op0, op1))
+
+    def tt(rd, wr, out, in0, in1, o):
+        op("v", rd, wr, lambda: V.tensor_tensor(out, in0, in1, o))
+
+    def cp(rd, wr, out, in_):
+        op("v", rd, wr, lambda: V.tensor_copy(out, in_))
+
+    def act(rd, wr, out, in_, func, bias=0.0, scale=1.0):
+        op("s", rd, wr, lambda: S.activation(out, in_, func, bias=bias, scale=scale))
+
+    def mm(rd, wr, out, pairs, start=True, stop=True):
+        n = len(pairs)
+        op("p", rd, wr, *[(lambda i=i: PE.matmul(out, pairs[i][0], pairs[i][1], start and i == 0, stop and i == n - 1)) for i in range(n)])
+
+    def sel(rd, wr, out, in_, pattern, cmp, fill, base):
+        op("g", rd, wr, lambda: g.affine_select(out, in_, pattern, cmp, fill, base, 1))
+
+    places = T.V[:, 0:W]
+    own, mate = [[-1, 128]], [[-2, 64], [1, 2]]
+
+    dma("y", "ltg", "", "tgi", (T.tgi[:], T.tg[:]))
+    dma("y", "lx", "", "V", (places, T.x[:]))
+    op("v", "", "zA", lambda: V.memset(T.zA[:], float(M + 32)))
+    op("v", "", "zB", lambda: V.memset(T.zB[:], float(M + 32 - 48)))
+    dma("s", "iA", "zA", "wA", (T.wA[0::16, :], T.zA[:]))
+    dma("s", "iB", "zB", "wB", (T.wB[0::16, :], T.zB[:]))
+    dma("s", "ltr", "", "tri", (T.tri[:], T.trig[:]))
+    dma("s", "lsr", "", "sri", (T.sri[:], T.src[:]))
+    dma("s", "lth", "", "thi", (T.thi[:], T.th[:]))
+    op("g", "", "pi", lambda: g.iota(T.pi[:], [[0, 1]], 0, 1))
+    op("g", "", "J", lambda: g.iota(T.J[:], [[1, 144]], -15, 0, allow_small_or_imprecise_dtypes=True))
+    op("g", "", "GB", lambda: g.iota(T.GB[:], [[16, 8], [0, 16]], 0, 0, allow_small_or_imprecise_dtypes=True))
+    op("g", "", "val", lambda: g.iota(T.val[:], [[1, 48], [KC, 16]], 32, 0, allow_small_or_imprecise_dtypes=True))
+    op("v", "", "SW", lambda: V.memset(T.SW[:], 0.0))
+    ts("pi", "gbi", T.gbi[:], T.pi[:], 112, A.bitwise_and)
+    cp("pi", "pf", T.pf[:], T.pi[:])
+    cp("gbi", "gbf", T.gbf[:], T.gbi[:])
+    ts("J gbf", "E", T.E[:], T.J[:], T.gbf[:], A.is_equal)
+    ts("pf gbf", "w1", T.w1[:], T.pf[:], T.gbf[:], A.is_equal, BIG - 1.0, A.mult)
+    ts("GB gbf", "OB", T.OB[:], T.GB[:], T.gbf[:], A.is_equal)
+    ts("GB gbf", "nOB", T.nOB[:], T.GB[:], T.gbf[:], A.is_equal, -1.0, A.mult)
+    ts("w1", "w2", T.w2[:], T.w1[:], 1.0, A.add)
+    ts("J gbf w2", "E2", T.E2[:], T.J[:], T.gbf[:], A.is_equal, T.w2[:], A.mult)
+    ts("tgi", "ci", T.ci[:], T.tgi[:], 8, A.logical_shift_right)
+    ts("tgi", "f1", T.f1[:], T.tgi[:], 13.0, A.mult)
+    ts("ci", "f2", T.f2[:], T.ci[:], -3327.0, A.mult)
+    cp("tgi", "ES0", T.ES0[:], T.tgi[:])
+    tt("f1 f2", "f3", T.f3[:], T.f1[:], T.f2[:], A.add)
+    cp("f3", "tpu", T.tpu[:], T.f3[:])
+    cp("val tpu", "wA", T.wA[:, 0:W].indirect(T.tpu[:, 0:48]), T.val[:])
+    op("s", "val tpu", "wB", lambda: S.activation(T.wB[:, 0:W].indirect(T.tpu[:, 48:96]), T.val[:], F.Silu))
+    dma("y", "oA", "wA", "uA", (T.uA[:], T.wA[0::16, :]))
+    dma("y", "oB", "wB", "uB", (T.uB[:], T.wB[0::16, :]))
+    sel("OB", "I", T.I[:], T.OB[:], own, A.is_equal, 0.0, 0)
+    sel("nOB", "nJ", T.nJ[:], T.nOB[:], own, A.is_equal, 0.0, 0)
+    send("E", 0, 0, "ES0", T.ES0[:])
+    sel("nOB", "Ua", T.Ua[:], T.nOB[:], own, A.is_gt, 0.0, 0)
+    sel("Ua", "U", T.U[:], T.Ua[:], own, A.not_equal, -2048.0, 0)
+    sel("OB", "Sw", T.Sw[:], T.OB[:], mate, A.is_equal, 0.0, -1)
+    sel("nOB", "Ub", T.Ub[:], T.nOB[:], mate, A.is_gt, 0.0, -1)
+    sel("Ub", "Um", T.Um[:], T.Ub[:], mate, A.not_equal, -2048.0, -1)
+    cp("tri", "tru", T.tru[:], T.tri[:])
+    cp("sri", "sru", T.sru[:], T.sri[:])
+    cp("thi", "thf", T.thf[:], T.thi[:])
+    cp("tgi", "tgf", T.tgf[:], T.tgi[:])
+    cp("sri", "srf", T.srf[:], T.sri[:])
+    cp("sri", "hi0", T.OS0[:, KC:2 * KC], T.sri[:])
+    cp("tri", "trf", T.trf[:], T.tri[:])
+    tt("srf hi0", "lo0", T.OS0[:, 2 * KC:3 * KC], T.srf[:], T.OS0[:, KC:2 * KC], A.subtract)
+
+    def amend_trigger(r):
+        ts("", "pH hit", T.hit[:], T.pH[:, 0:KC], BIG, A.is_ge)
+        tt("hit d1", "f1", T.f1[:], T.hit[:], T.d1[:], A.mult)
+        tt("f1", "trf", T.trf[:], T.f1[:], T.trf[:], A.add)
+        if r < RO:
+            cp("trf", "tru", T.tru[:], T.trf[:])
+        par = [(T.I[:], T.hit[:]), (T.Sw[:], T.hit[:])] + ([(T.I[:], T.pb[:])] if r > 1 else [])
+        mm("I Sw hit pb", "pM", T.pM[:, 0:KC], par)
+        mm("If nI srf hit", "pM", T.pM[:, KC:2 * KC], [(T.If[:], T.srf[:]), (T.nI[:], T.hit[:])])
+        act("", "pH Af", T.Af[:], T.pH[:, 0:KC], F.Relu, bias=-BIG)
+        act("", "pM x1", T.x1[:], T.pM[:, 0:KC], F.Abs, bias=-1.0)
+        act("x1", "pb", T.pb[:], T.x1[:], F.Abs, bias=-1.0)
+        if r < RO:
+            act("pb", "thr0", T.thr[:, 0:KC], T.pb[:], F.Identity, bias=TH, scale=-8192.0)
+            act("pb", "thr1", T.thr[:, KC:2 * KC], T.pb[:], F.Identity, bias=TH - 8192.0, scale=8192.0)
+
+    def amend_target(r):
+        tt("pb", "pC f2", T.f2[:], T.pC[:, 0:KC], T.pb[:], A.mult)
+        tt("f2", "pC tgf", T.tgf[:], T.pC[:, KC:2 * KC], T.f2[:], A.add)
+        if r < RO:
+            cp("tgf", "ES%d" % r, T["ES%d" % r][:], T.tgf[:])
+            send("E", r, 0, "ES%d" % r, T["ES%d" % r][:])
+
+    def amend_source(r):
+        tt("Af", "pM srf", T.srf[:], T.pM[:, KC:2 * KC], T.Af[:], A.max)
+        if r < RO:
+            cp("srf", "sru", T.sru[:], T.srf[:])
+            tt("srf pb", "f3", T.f3[:], T.srf[:], T.pb[:], A.mult)
+
+    def masks(c):
+        a, b, q, bank = DCH[c]
+        mm("nJ V", bank, T[bank][:, 0:16 * (b - a)], [(T.nJ[:], T.V[:, P + 16 * a:P + 16 * b])], stop=False)
+
+    def watched(c):
+        a, b, q, bank = DCH[c]
+        out, at = T.B[:, 16 * a:16 * b], places.indirect(T.tru[:, a:b])
+        if q == "v":
+            cp("V tru", "B%d" % c, out, at)
+        else:
+            act("V tru", "B%d" % c, out, at, F.Identity)
+        mm("I B%d" % c, bank, T[bank][:, 0:16 * (b - a)], [(T.I[:], out)], start=False)
+
+    def distance(c):
+        a, b, q, bank = DCH[c]
+        act("", "%s D%d" % (bank, c), T.D[:, 16 * a:16 * b], T[bank][:, 0:16 * (b - a)], F.Abs)
+        mm("E D%d" % c, "pF", T.pF[:, a:b], [(T.E[:, 15 - i:143 - i], T.D[:, 16 * a + i:16 * b:16]) for i in range(16)])
+
+    def message(r, c):
+        a, b = MCH[c]
+        out = T["mS%d" % r][:, 16 * a:16 * b]
+        tt("V sru K%d" % c, "m%d_%d" % (r, c), out, places.indirect(T.sru[:, a:b]), T.K[:, 16 * a:16 * b], A.max)
+        send("m", r, c, "m%d_%d" % (r, c), out)
+
+    def old(r, c):
+        a, b = MCH[c]
+        act("V aE%d" % r, "Y%d" % c, T.Y[:, 16 * a:16 * b], places.indirect(T["EL%d" % r][:, a:b]), F.Identity, bias=-8.0, scale=0.5)
+        mm("I Y%d" % c, "pT%d" % c, T["pT%d" % c][:], [(T.I[:], T.Y[:, 16 * a:16 * b])], stop=False)
+
+    def merge(r, c):
+        a, b = MCH[c]
+        mm("I am%d_%d" % (r, c), "pT%d" % c, T["pT%d" % c][:], [(T.I[:], T["mL%d" % r][:, 16 * a:16 * b])], start=False)
+        act("", "pT%d T%d" % (c, c), T.Tt[:, 16 * a:16 * b], T["pT%d" % c][:], F.Abs, bias=-15.0)
+
+    for r in range(RO):
+        OS, GSn = T["OS%d" % r], T["GS%d" % r]
+        masks(0)
+        masks(1)
+        if r:
+            amend_trigger(r)
+        masks(2)
+        masks(3)
+        watched(0)
+        watched(1)
+        distance(0)
+        distance(1)
+        if r:
+            amend_target(r)
+        watched(2)
+        distance(2)
+        watched(3)
+        distance(3)
+        if r:
+            amend_source(r)
+        ts("V", "K0", T.K[:, 0:512], T.V[:, P:P + 512], 8.0, A.is_lt, 31.0, A.mult)
+        message(r, 0)
+        ts("thf", "pF cb", T.cb[:], T.pF[:, 0:KC], T.thf[:], A.is_lt)
+        op("v", "cb", "Pb", lambda: V.tensor_tensor_scan(T.Pb[:], T.cb[:], T.cb[:], 0.0, A.add, A.max))
+        mm("OB U cb Pb", "pZ", T.pZ[:, 0:KC], [(T.U[:], T.cb[:]), (T.OB[:], T.Pb[:])])
+        if r:
+            mm("OB Um cb Pb", "pZ", T.pZ[:, KC:2 * KC], [(T.Um[:], T.cb[:]), (T.OB[:], T.Pb[:])])
+            mm("If SI srf f3", "pM", T.pM[:, 2 * KC:3 * KC], [(T.If[:], T.srf[:]), (T.SI[:], T.f3[:])])
+            act("", "pM hi%d" % r, OS[:, KC:2 * KC], T.pM[:, 2 * KC:3 * KC], F.Identity)
+        ts("", "pZ f4", T.f4[:], T.pZ[:, 0:KC], TH, A.is_gt, float(W), A.mult)
+        tt("f4 tgf", "f5", T.f5[:], T.f4[:], T.tgf[:], A.add)
+        cp("f5", "G%d" % r, GSn[:], T.f5[:])
+        send("G", r, 0, "G%d" % r, GSn[:])
+        if r:
+            tt("thr0 thr1", "pZ G2", T.G2[:], T.pZ[:, 0:2 * KC], T.thr[:], A.is_le)
+            tt("hi%d" % r, "pM lo%d" % r, OS[:, 2 * KC:3 * KC], T.pM[:, 2 * KC:3 * KC], OS[:, KC:2 * KC], A.subtract)
+            tt("G2", "go%d" % r, OS[:, 0:KC], T.G2[:, 0:KC], T.G2[:, KC:2 * KC], A.add)
+        else:
+            ts("", "pZ go0", OS[:, 0:KC], T.pZ[:, 0:KC], TH, A.is_le)
+        send("O", r, 0, "go%d hi%d lo%d" % (r, r, r), OS[:])
+        ts("V", "K1 K2", T.K[:, 512:M], T.V[:, P + 512:W], 8.0, A.is_lt, 31.0, A.mult)
+        if r == 0:
+            ts("uB", "i1", T.i1[:], T.uB[:, :, 7:13], 48.0, A.add)
+            tt("uA i1", "i2", T.i2[:], T.uA[:, :, 7:13], T.i1[:], A.min)
+            ts("i2", "i3", T.i3[:], T.i2[:], -32.0, A.add)
+            cp("i3", "invS", T.invS[:], T.i3[:])
+            send("I", 0, 0, "invS", T.invS[:])
+        message(r, 1)
+        message(r, 2)
+        tt("srf trf", "d1", T.d1[:], T.srf[:], T.trf[:], A.subtract)
+        if r == 0:
+            cp("I", "If", T.If[:], T.I[:])
+            tt("I Sw", "SI", T.SI[:], T.Sw[:], T.I[:], A.subtract)
+            ts("I", "nI", T.nI[:], T.I[:], -BIG, A.mult)
+        OL = T["OL%d" % r]
+        dma("y", "fl%d" % r, "aO%d" % r, "SW", *[(T.SW[i::16, 0:M], OL[:, i * KC:(i + 1) * KC]) for i in range(3)])
+        old(r, 0)
+        merge(r, 0)
+        old(r, 1)
+        old(r, 2)
+        merge(r, 1)
+        merge(r, 2)
+        if r == 0:
+            mm("SI tgf", "pC", T.pC[:, 0:KC], [(T.SI[:], T.tgf[:])])
+            mm("If tgf", "pC", T.pC[:, KC:2 * KC], [(T.If[:], T.tgf[:])])
+        for c in range(3):
+            a, b = MCH[c]
+            tt("Y%d T%d aG%d" % (c, c, r), "V", T.V[:, 0:2 * W].indirect(T["GL%d" % r][:, a:b]),
+               T.Y[:, 16 * a:16 * b], T.Tt[:, 16 * a:16 * b], A.add)
+        for c, (a, b) in enumerate(SCH):
+            act("SW aI", "S%d" % c, T.GS[:, 16 * a:16 * b], T.SW[:, 0:M + 16].indirect(T.invL[:, a:b]), F.Identity)
+            mm("E2 S%d" % c, "pH", T.pH[:, 0:KC],
+               [(T.E2[:, 15 - i:143 - i], T.GS[:, KC * i:KC * (i + 1)]) for i in range(a // 6, b // 6)], start=c == 0, stop=c == len(SCH) - 1)
+
+    dma("y", "ox", "V", "", (T.yx[:], places))
+    amend_trigger(RO)
+    amend_source(RO)
+    amend_target(RO)
+    dma("s", "ol", "trf srf tgf", "", (T.ytrig[:], T.trf[:]), (T.ysrc[:], T.srf[:]), (T.ytg[:], T.tgf[:]))
+    for name, val in total.items():
+        if seen["g"].get(name, 0) < val:
+            g.wait_ge(T.sem[name], val)

@@ -4,8 +4,9 @@ N, P, M, W, CAP, STEP, RO = 8, 1792, 1536, 3328, 768, 3, 3
 KC = M // 16
 BIG = 4096.0
 TH = float(CAP - 2048)
-DCH = [(72, 96, "s", "pT2"), (0, 32, "v", "pT0"), (32, 56, "v", "pT1"), (56, 72, "v", "pZ")]
+DCH = [(0, 32, "v", "pT0"), (32, 64, "s", "pT1"), (64, 96, "s", "pT2")]
 MCH = [(0, 32), (32, 64), (64, 96)]
+MORD = [1, 0, 2]
 SCH = [(0, 24), (24, 48), (48, 72), (72, 96)]
 
 SCRATCH = {
@@ -43,17 +44,23 @@ for _r in range(RO):
         SCRATCH["m%s%d" % (_s, _r)] = ("sbuf", [128, M], "bfloat16")
         SCRATCH["E%s%d" % (_s, _r)] = ("sbuf", [128, KC], "uint16")
         SCRATCH["G%s%d" % (_s, _r)] = ("sbuf", [128, KC], "uint16")
-        SCRATCH["O%s%d" % (_s, _r)] = ("sbuf", [128, 3 * KC], "bfloat16")
-    SEMAPHORES += ["aE%d" % _r, "aG%d" % _r, "aO%d" % _r, "fl%d" % _r] + ["am%d_%d" % (_r, _c) for _c in range(3)]
+        SCRATCH["O%s%d" % (_s, _r)] = ("sbuf", [128, KC], "bfloat16")
+        SCRATCH["B%s%d" % (_s, _r)] = ("sbuf", [128, 2 * KC], "bfloat16")
+    SEMAPHORES += ["aE%d" % _r, "aG%d" % _r, "aO%d" % _r, "aB%d" % _r, "fl%d" % _r, "fb%d" % _r] + ["am%d_%d" % (_r, _c) for _c in range(3)]
 
 
-def helpers(T, topo, q):
+def via(T, topo, q, kind, c):
     a, b = T.cores[q], T.cores[(q + STEP) % N]
+    free = [k for k in topo.cores_of(a) if topo.may_write(k, b) and T.rank_of(k) is None]
+    near = [k for k in free if topo.die(k) == topo.die(a)]
+    far = [k for k in free if topo.die(k) != topo.die(a)]
+    if kind == "B":
+        return far[1]
+    if (kind, c) == ("m", 0):
+        return far[0]
     if topo.may_write(a, b):
         return None
-    c = [k for k in topo.cores_of(a) if topo.may_write(k, b) and T.rank_of(k) is None]
-    c.sort(key=lambda k: topo.die(k) != topo.die(a))
-    return c[0], c[1]
+    return near[1 if kind == "m" else 0]
 
 
 def landing(T, kind, r, c):
@@ -70,29 +77,29 @@ def write(g, T, topo, me, to, out, in_, sem):
     return len(topo.engines(me, to))
 
 
-def hand_on(g, core, T, topo, q, lists):
+def hand_on(g, core, T, topo, q):
     a, b = T.cores[q], T.cores[(q + STEP) % N]
     n, sent = len(topo.engines(a, core)), 0
     for r in range(RO):
-        order = [("E", 0), ("G", 0), ("O", 0)] + ([("I", 0)] if r == 0 else []) if lists else [("m", c) for c in range(3)]
+        order = [("E", 0), ("B", 0), ("G", 0), ("O", 0)] + ([("I", 0)] if r == 0 else []) + [("m", c) for c in range(3)]
         for kind, c in order:
-            ap, sem = landing(T, kind, r, c)
-            g.wait_ge(T.sem[sem], n)
-            sent += write(g, T, topo, core, b, ap, ap, sem)
-    g.wait_ge(T.sem.sent, sent)
+            if via(T, topo, q, kind, c) == core:
+                ap, sem = landing(T, kind, r, c)
+                g.wait_ge(T.sem[sem], n)
+                sent += write(g, T, topo, core, b, ap, ap, sem)
+    if sent:
+        g.wait_ge(T.sem.sent, sent)
 
 
 def rank_program(g, core, T, topo):
     rank = T.rank_of(core)
     if rank is None:
         for q in range(N):
-            h = helpers(T, topo, q)
-            if h is not None and core in h:
-                hand_on(g, core, T, topo, q, core == h[0])
+            if core in topo.cores_of(T.cores[q]):
+                hand_on(g, core, T, topo, q)
         return
 
     nxt, prv = T.cores[(rank + STEP) % N], (rank - STEP) % N
-    h_out, h_in = helpers(T, topo, rank), helpers(T, topo, prv)
     Q = {"v": g.vector, "s": g.scalar, "p": g.tensor, "g": g, "y": g.sync}
     V, S, PE = g.vector, g.scalar, g.tensor
     total, seen, lastw, readers = {}, {q: {} for q in Q}, {}, {}
@@ -146,10 +153,9 @@ def rank_program(g, core, T, topo):
     def send(kind, r, c, rd, in_):
         before("g", rd.split(), [])
         ap, sem = landing(T, kind, r, c)
-        to = nxt if h_out is None else h_out[1 if kind == "m" else 0]
-        total["sent"] = total.get("sent", 0) + write(g, T, topo, core, to, ap, in_, sem)
-        frm = T.cores[prv] if h_in is None else h_in[1 if kind == "m" else 0]
-        total[sem] = len(topo.engines(frm, core))
+        to, frm = via(T, topo, rank, kind, c), via(T, topo, prv, kind, c)
+        total["sent"] = total.get("sent", 0) + write(g, T, topo, core, nxt if to is None else to, ap, in_, sem)
+        total[sem] = len(topo.engines(T.cores[prv] if frm is None else frm, core))
         lastw[sem] = (sem, total[sem], {})
 
     def ts(rd, wr, out, in0, s1, op0, s2=None, op1=None):
@@ -190,7 +196,7 @@ def rank_program(g, core, T, topo):
     op("g", "", "J", lambda: g.iota(T.J[:], [[1, 144]], -15, 0, allow_small_or_imprecise_dtypes=True))
     op("g", "", "GB", lambda: g.iota(T.GB[:], [[16, 8], [0, 16]], 0, 0, allow_small_or_imprecise_dtypes=True))
     op("g", "", "val", lambda: g.iota(T.val[:], [[1, 48], [KC, 16]], 32, 0, allow_small_or_imprecise_dtypes=True))
-    op("v", "", "SW", lambda: V.memset(T.SW[:], 0.0))
+    op("v", "", "SWa SWb", lambda: V.memset(T.SW[:], 0.0))
     ts("pi", "gbi", T.gbi[:], T.pi[:], 112, A.bitwise_and)
     cp("pi", "pf", T.pf[:], T.pi[:])
     cp("gbi", "gbf", T.gbf[:], T.gbi[:])
@@ -220,12 +226,12 @@ def rank_program(g, core, T, topo):
     sel("Ub", "Um", T.Um[:], T.Ub[:], mate, A.not_equal, -2048.0, -1)
     cp("tri", "tru", T.tru[:], T.tri[:])
     cp("sri", "sru", T.sru[:], T.sri[:])
-    cp("thi", "thf", T.thf[:], T.thi[:])
-    cp("tgi", "tgf", T.tgf[:], T.tgi[:])
     cp("sri", "srf", T.srf[:], T.sri[:])
-    cp("sri", "hi0", T.OS0[:, KC:2 * KC], T.sri[:])
-    cp("tri", "trf", T.trf[:], T.tri[:])
-    tt("srf hi0", "lo0", T.OS0[:, 2 * KC:3 * KC], T.srf[:], T.OS0[:, KC:2 * KC], A.subtract)
+    cp("sri", "hi0", T.BS0[:, 0:KC], T.sri[:])
+    cp("thi", "thf", T.thf[:], T.thi[:])
+    tt("srf hi0", "lo0", T.BS0[:, KC:2 * KC], T.srf[:], T.BS0[:, 0:KC], A.subtract)
+    cp("tgi", "tgf", T.tgf[:], T.tgi[:])
+    send("B", 0, 0, "hi0 lo0", T.BS0[:])
 
     def amend_trigger(r):
         ts("", "pH hit", T.hit[:], T.pH[:, 0:KC], BIG, A.is_ge)
@@ -239,9 +245,6 @@ def rank_program(g, core, T, topo):
         act("", "pH Af", T.Af[:], T.pH[:, 0:KC], F.Relu, bias=-BIG)
         act("", "pM x1", T.x1[:], T.pM[:, 0:KC], F.Abs, bias=-1.0)
         act("x1", "pb", T.pb[:], T.x1[:], F.Abs, bias=-1.0)
-        if r < RO:
-            act("pb", "thr0", T.thr[:, 0:KC], T.pb[:], F.Identity, bias=TH, scale=-8192.0)
-            act("pb", "thr1", T.thr[:, KC:2 * KC], T.pb[:], F.Identity, bias=TH - 8192.0, scale=8192.0)
 
     def amend_target(r):
         tt("pb", "pC f2", T.f2[:], T.pC[:, 0:KC], T.pb[:], A.mult)
@@ -277,6 +280,7 @@ def rank_program(g, core, T, topo):
     def message(r, c):
         a, b = MCH[c]
         out = T["mS%d" % r][:, 16 * a:16 * b]
+        ts("V", "K%d" % c, T.K[:, 16 * a:16 * b], T.V[:, P + 16 * a:P + 16 * b], 8.0, A.is_lt, 31.0, A.mult)
         tt("V sru K%d" % c, "m%d_%d" % (r, c), out, places.indirect(T.sru[:, a:b]), T.K[:, 16 * a:16 * b], A.max)
         send("m", r, c, "m%d_%d" % (r, c), out)
 
@@ -291,76 +295,76 @@ def rank_program(g, core, T, topo):
         act("", "pT%d T%d" % (c, c), T.Tt[:, 16 * a:16 * b], T["pT%d" % c][:], F.Abs, bias=-15.0)
 
     for r in range(RO):
-        OS, GSn = T["OS%d" % r], T["GS%d" % r]
+        OS, BS, GSn = T["OS%d" % r], T["BS%d" % r], T["GS%d" % r]
         masks(0)
         masks(1)
         if r:
             amend_trigger(r)
         masks(2)
-        masks(3)
         watched(0)
         watched(1)
-        distance(0)
-        distance(1)
         if r:
             amend_target(r)
-        watched(2)
-        distance(2)
-        watched(3)
-        distance(3)
-        if r:
             amend_source(r)
-        ts("V", "K0", T.K[:, 0:512], T.V[:, P:P + 512], 8.0, A.is_lt, 31.0, A.mult)
+            mm("If SI srf f3", "pM", T.pM[:, 2 * KC:3 * KC], [(T.If[:], T.srf[:]), (T.SI[:], T.f3[:])])
+        watched(2)
+        distance(0)
+        distance(1)
+        distance(2)
         message(r, 0)
+        if r:
+            cp("", "pM hi%d" % r, BS[:, 0:KC], T.pM[:, 2 * KC:3 * KC])
+            tt("hi%d" % r, "pM lo%d" % r, BS[:, KC:2 * KC], T.pM[:, 2 * KC:3 * KC], BS[:, 0:KC], A.subtract)
+            send("B", r, 0, "hi%d lo%d" % (r, r), BS[:])
+            act("pb", "thr0", T.thr[:, 0:KC], T.pb[:], F.Identity, bias=TH, scale=-8192.0)
+            act("pb", "thr1", T.thr[:, KC:2 * KC], T.pb[:], F.Identity, bias=TH - 8192.0, scale=8192.0)
+        message(r, 1)
         ts("thf", "pF cb", T.cb[:], T.pF[:, 0:KC], T.thf[:], A.is_lt)
         op("v", "cb", "Pb", lambda: V.tensor_tensor_scan(T.Pb[:], T.cb[:], T.cb[:], 0.0, A.add, A.max))
         mm("OB U cb Pb", "pZ", T.pZ[:, 0:KC], [(T.U[:], T.cb[:]), (T.OB[:], T.Pb[:])])
         if r:
             mm("OB Um cb Pb", "pZ", T.pZ[:, KC:2 * KC], [(T.Um[:], T.cb[:]), (T.OB[:], T.Pb[:])])
-            mm("If SI srf f3", "pM", T.pM[:, 2 * KC:3 * KC], [(T.If[:], T.srf[:]), (T.SI[:], T.f3[:])])
-            act("", "pM hi%d" % r, OS[:, KC:2 * KC], T.pM[:, 2 * KC:3 * KC], F.Identity)
         ts("", "pZ f4", T.f4[:], T.pZ[:, 0:KC], TH, A.is_gt, float(W), A.mult)
         tt("f4 tgf", "f5", T.f5[:], T.f4[:], T.tgf[:], A.add)
         cp("f5", "G%d" % r, GSn[:], T.f5[:])
         send("G", r, 0, "G%d" % r, GSn[:])
         if r:
             tt("thr0 thr1", "pZ G2", T.G2[:], T.pZ[:, 0:2 * KC], T.thr[:], A.is_le)
-            tt("hi%d" % r, "pM lo%d" % r, OS[:, 2 * KC:3 * KC], T.pM[:, 2 * KC:3 * KC], OS[:, KC:2 * KC], A.subtract)
-            tt("G2", "go%d" % r, OS[:, 0:KC], T.G2[:, 0:KC], T.G2[:, KC:2 * KC], A.add)
+            tt("G2", "go%d" % r, OS[:], T.G2[:, 0:KC], T.G2[:, KC:2 * KC], A.add)
         else:
-            ts("", "pZ go0", OS[:, 0:KC], T.pZ[:, 0:KC], TH, A.is_le)
-        send("O", r, 0, "go%d hi%d lo%d" % (r, r, r), OS[:])
-        ts("V", "K1 K2", T.K[:, 512:M], T.V[:, P + 512:W], 8.0, A.is_lt, 31.0, A.mult)
+            ts("", "pZ go0", OS[:], T.pZ[:, 0:KC], TH, A.is_le)
+        send("O", r, 0, "go%d" % r, OS[:])
         if r == 0:
             ts("uB", "i1", T.i1[:], T.uB[:, :, 7:13], 48.0, A.add)
             tt("uA i1", "i2", T.i2[:], T.uA[:, :, 7:13], T.i1[:], A.min)
             ts("i2", "i3", T.i3[:], T.i2[:], -32.0, A.add)
             cp("i3", "invS", T.invS[:], T.i3[:])
             send("I", 0, 0, "invS", T.invS[:])
-        message(r, 1)
         message(r, 2)
-        tt("srf trf", "d1", T.d1[:], T.srf[:], T.trf[:], A.subtract)
         if r == 0:
+            cp("tri", "trf", T.trf[:], T.tri[:])
             cp("I", "If", T.If[:], T.I[:])
             tt("I Sw", "SI", T.SI[:], T.Sw[:], T.I[:], A.subtract)
             ts("I", "nI", T.nI[:], T.I[:], -BIG, A.mult)
-        OL = T["OL%d" % r]
-        dma("y", "fl%d" % r, "aO%d" % r, "SW", *[(T.SW[i::16, 0:M], OL[:, i * KC:(i + 1) * KC]) for i in range(3)])
-        old(r, 0)
-        merge(r, 0)
-        old(r, 1)
-        old(r, 2)
-        merge(r, 1)
-        merge(r, 2)
+        tt("srf trf", "d1", T.d1[:], T.srf[:], T.trf[:], A.subtract)
+        OL, BL = T["OL%d" % r], T["BL%d" % r]
+        rows = [lambda: dma("y", "fl%d" % r, "aO%d" % r, "SWa", (T.SW[0::16, 0:M], OL[:])),
+                lambda: dma("y", "fb%d" % r, "aB%d" % r, "SWb", *[(T.SW[1 + i::16, 0:M], BL[:, i * KC:(i + 1) * KC]) for i in range(2)])]
+        for f in (rows if r else rows[::-1]):
+            f()
+        for c in MORD:
+            old(r, c)
+        for c in MORD:
+            merge(r, c)
         if r == 0:
             mm("SI tgf", "pC", T.pC[:, 0:KC], [(T.SI[:], T.tgf[:])])
             mm("If tgf", "pC", T.pC[:, KC:2 * KC], [(T.If[:], T.tgf[:])])
-        for c in range(3):
+        for c in MORD:
             a, b = MCH[c]
             tt("Y%d T%d aG%d" % (c, c, r), "V", T.V[:, 0:2 * W].indirect(T["GL%d" % r][:, a:b]),
                T.Y[:, 16 * a:16 * b], T.Tt[:, 16 * a:16 * b], A.add)
         for c, (a, b) in enumerate(SCH):
-            act("SW aI", "S%d" % c, T.GS[:, 16 * a:16 * b], T.SW[:, 0:M + 16].indirect(T.invL[:, a:b]), F.Identity)
+            act("SWa SWb aI", "S%d" % c, T.GS[:, 16 * a:16 * b], T.SW[:, 0:M + 16].indirect(T.invL[:, a:b]), F.Identity)
             mm("E2 S%d" % c, "pH", T.pH[:, 0:KC],
                [(T.E2[:, 15 - i:143 - i], T.GS[:, KC * i:KC * (i + 1)]) for i in range(a // 6, b // 6)], start=c == 0, stop=c == len(SCH) - 1)
 

from concourse.mybir import AluOpType as A, ActivationFunctionType as F

N, P, M, W, CAP, STEP, RO = 8, 1792, 1536, 3328, 768, 3, 3
KC = M // 16
BIG = 4096.0
TH = float(CAP - 2048)
DCH = [(0, 32, "v", "pT0"), (32, 64, "s", "pT1"), (64, 96, "s", "pT2")]
MCH = [(0, 32), (32, 64), (64, 96)]
MORD = [1, 0, 2]
SCH = [(0, 24), (24, 48), (48, 72), (72, 96)]

SCRATCH = {
    "V": ("sbuf", [128, 2 * W], "bfloat16"), "B": ("sbuf", [128, M], "bfloat16"),
    "D": ("sbuf", [128, M], "bfloat16"), "K": ("sbuf", [128, M], "bfloat16"), "Y": ("sbuf", [128, M], "bfloat16"),
    "Tt": ("sbuf", [128, M], "bfloat16"), "GS": ("sbuf", [128, M], "bfloat16"), "SW": ("sbuf", [128, M + 16], "bfloat16"),
    "wA": ("sbuf", [128, W], "float32"), "wB": ("sbuf", [128, W], "float32"), "val": ("sbuf", [128, M // 2], "float32"),
    "zA": ("sbuf", [128, 208], "float32"), "zB": ("sbuf", [128, 208], "float32"),
    "uA": ("sbuf", [128, 16, 13], "float32"), "uB": ("sbuf", [128, 16, 13], "float32"),
    "i1": ("sbuf", [128, 16, 6], "float32"), "i2": ("sbuf", [128, 16, 6], "float32"), "i3": ("sbuf", [128, 16, 6], "int32"),
    "invS": ("sbuf", [128, KC], "uint16"), "invL": ("sbuf", [128, KC], "uint16"),
    "tgi": ("sbuf", [128, KC], "int32"), "tri": ("sbuf", [128, KC], "int32"), "sri": ("sbuf", [128, KC], "int32"),
    "thi": ("sbuf", [128, 1], "int32"), "thf": ("sbuf", [128, 1], "float32"),
    "ci": ("sbuf", [128, KC], "int32"), "tpu": ("sbuf", [128, KC], "uint16"),
    "tru": ("sbuf", [128, KC], "uint16"), "sru": ("sbuf", [128, KC], "uint16"),
    "G2": ("sbuf", [128, 2 * KC], "bfloat16"), "thr": ("sbuf", [128, 2 * KC], "float32"),
    "J": ("sbuf", [128, 144], "float32"), "GB": ("sbuf", [128, 128], "float32"),
    "pi": ("sbuf", [128, 1], "int32"), "gbi": ("sbuf", [128, 1], "int32"),
    "E": ("sbuf", [128, 144], "bfloat16"), "E2": ("sbuf", [128, 144], "bfloat16"),
    "If": ("sbuf", [128, 128], "float32"), "SI": ("sbuf", [128, 128], "float32"),
}
for _n in ("pf", "gbf", "w1", "w2"):
    SCRATCH[_n] = ("sbuf", [128, 1], "float32")
for _n in ("nJ", "I", "Sw", "nI", "OB", "nOB", "Ua", "U", "Ub", "Um"):
    SCRATCH[_n] = ("sbuf", [128, 128], "bfloat16")
for _n in ("trf", "srf", "tgf", "d1", "f1", "f2", "f3", "f4", "f5", "Af", "x1"):
    SCRATCH[_n] = ("sbuf", [128, KC], "float32")
for _n in ("cb", "Pb", "hit", "pb"):
    SCRATCH[_n] = ("sbuf", [128, KC], "bfloat16")
for _n in ("pT0", "pT1", "pT2", "pF", "pZ", "pH", "pM", "pC"):
    SCRATCH[_n] = ("psum", [128, 512], "float32")
SEMAPHORES = ["sv", "ss", "sp", "sg", "ltg", "lx", "ltr", "lsr", "lth", "iA", "iB", "oA", "oB", "ox", "ol", "sent", "aI"]
for _r in range(RO):
    for _s in "SL":
        SCRATCH["m%s%d" % (_s, _r)] = ("sbuf", [128, M], "bfloat16")
        SCRATCH["E%s%d" % (_s, _r)] = ("sbuf", [128, KC], "uint16")
        SCRATCH["G%s%d" % (_s, _r)] = ("sbuf", [128, KC], "uint16")
        SCRATCH["O%s%d" % (_s, _r)] = ("sbuf", [128, KC], "bfloat16")
        SCRATCH["B%s%d" % (_s, _r)] = ("sbuf", [128, 2 * KC], "bfloat16")
    SEMAPHORES += ["aE%d" % _r, "aG%d" % _r, "aO%d" % _r, "aB%d" % _r, "fl%d" % _r, "fb%d" % _r] + ["am%d_%d" % (_r, _c) for _c in range(3)]


def via(T, topo, q, kind, c):
    a, b = T.cores[q], T.cores[(q + STEP) % N]
    free = [k for k in topo.cores_of(a) if topo.may_write(k, b) and T.rank_of(k) is None]
    near = [k for k in free if topo.die(k) == topo.die(a)]
    far = [k for k in free if topo.die(k) != topo.die(a)]
    if kind == "B":
        return far[1]
    if (kind, c) == ("m", 0):
        return far[0]
    if topo.may_write(a, b):
        return None
    return near[1 if kind == "m" else 0]


def landing(T, kind, r, c):
    if kind == "I":
        return T.invL[:], "aI"
    if kind == "m":
        return T["mL%d" % r][:, 16 * MCH[c][0]:16 * MCH[c][1]], "am%d_%d" % (r, c)
    return T["%sL%d" % (kind, r)][:], "a%s%d" % (kind, r)


def write(g, T, topo, me, to, out, in_, sem):
    rid, pid = topo.addr(to, me)
    g.remote_dma(out, in_, T.sem[sem], T.sem.sent, pid, rid, topo.mask(me, to))
    return len(topo.engines(me, to))


def hand_on(g, core, T, topo, q):
    a, b = T.cores[q], T.cores[(q + STEP) % N]
    n, sent = len(topo.engines(a, core)), 0
    for r in range(RO):
        order = [("E", 0), ("B", 0), ("G", 0), ("O", 0)] + ([("I", 0)] if r == 0 else []) + [("m", c) for c in range(3)]
        for kind, c in order:
            if via(T, topo, q, kind, c) == core:
                ap, sem = landing(T, kind, r, c)
                g.wait_ge(T.sem[sem], n)
                sent += write(g, T, topo, core, b, ap, ap, sem)
    if sent:
        g.wait_ge(T.sem.sent, sent)


def rank_program(g, core, T, topo):
    rank = T.rank_of(core)
    if rank is None:
        for q in range(N):
            if core in topo.cores_of(T.cores[q]):
                hand_on(g, core, T, topo, q)
        return

    nxt, prv = T.cores[(rank + STEP) % N], (rank - STEP) % N
    Q = {"v": g.vector, "s": g.scalar, "p": g.tensor, "g": g, "y": g.sync}
    V, S, PE = g.vector, g.scalar, g.tensor
    total, seen, lastw, readers = {}, {q: {} for q in Q}, {}, {}

    def need(q, evs):
        for name, val, snap in sorted(evs, key=lambda e: -len(e[2])):
            if q == "p" and name == "sp":
                continue
            if seen[q].get(name, 0) < val:
                Q[q].wait_ge(T.sem[name], val)
                seen[q][name] = val
                for k, v in snap.items():
                    if seen[q].get(k, 0) < v:
                        seen[q][k] = v

    def before(q, rd, wr):
        evs = [lastw[k] for k in rd + wr if k in lastw]
        for k in wr:
            evs += readers.get(k, [])
        best = {}
        for e in evs:
            if e[0] not in best or best[e[0]][1] < e[1]:
                best[e[0]] = e
        need(q, list(best.values()))

    def after(ev, rd, wr):
        for k in rd:
            readers.setdefault(k, []).append(ev)
        for k in wr:
            lastw[k] = ev
            readers[k] = []

    def op(q, rd, wr, *fns):
        rd, wr = rd.split(), wr.split()
        before(q, rd, wr)
        for fn in fns:
            ins = fn()
        name = "s" + q
        ins.then_inc(T.sem[name], 1)
        total[name] = total.get(name, 0) + 1
        after((name, total[name], dict(seen[q])), rd, wr)

    def dma(q, name, rd, wr, *pairs):
        rd, wr = rd.split(), wr.split()
        before(q, rd, wr)
        for out, in_ in pairs:
            Q[q].dma_start(out, in_).then_inc(T.sem[name], 16)
            total[name] = total.get(name, 0) + 16
        after((name, total[name], dict(seen[q])), rd, wr)

    def send(kind, r, c, rd, in_):
        before("g", rd.split(), [])
        ap, sem = landing(T, kind, r, c)
        to, frm = via(T, topo, rank, kind, c), via(T, topo, prv, kind, c)
        total["sent"] = total.get("sent", 0) + write(g, T, topo, core, nxt if to is None else to, ap, in_, sem)
        total[sem] = len(topo.engines(T.cores[prv] if frm is None else frm, core))
        lastw[sem] = (sem, total[sem], {})

    def ts(rd, wr, out, in0, s1, op0, s2=None, op1=None):
        if op1 is None:
            op("v", rd, wr, lambda: V.tensor_scalar(out, in0, s1, None, op0))
        else:
            op("v", rd, wr, lambda: V.tensor_scalar(out, in0, s1, s2, op0, op1))

    def tt(rd, wr, out, in0, in1, o):
        op("v", rd, wr, lambda: V.tensor_tensor(out, in0, in1, o))

    def cp(rd, wr, out, in_):
        op("v", rd, wr, lambda: V.tensor_copy(out, in_))

    def act(rd, wr, out, in_, func, bias=0.0, scale=1.0):
        op("s", rd, wr, lambda: S.activation(out, in_, func, bias=bias, scale=scale))

    def mm(rd, wr, out, pairs, start=True, stop=True):
        n = len(pairs)
        op("p", rd, wr, *[(lambda i=i: PE.matmul(out, pairs[i][0], pairs[i][1], start and i == 0, stop and i == n - 1)) for i in range(n)])

    def sel(rd, wr, out, in_, pattern, cmp, fill, base):
        op("g", rd, wr, lambda: g.affine_select(out, in_, pattern, cmp, fill, base, 1))

    places = T.V[:, 0:W]
    own, mate = [[-1, 128]], [[-2, 64], [1, 2]]

    dma("y", "ltg", "", "tgi", (T.tgi[:], T.tg[:]))
    dma("y", "lx", "", "V", (places, T.x[:]))
    op("v", "", "zA", lambda: V.memset(T.zA[:], float(M + 32)))
    op("v", "", "zB", lambda: V.memset(T.zB[:], float(M + 32 - 48)))
    dma("s", "iA", "zA", "wA", (T.wA[0::16, :], T.zA[:]))
    dma("s", "iB", "zB", "wB", (T.wB[0::16, :], T.zB[:]))
    dma("s", "ltr", "", "tri", (T.tri[:], T.trig[:]))
    dma("s", "lsr", "", "sri", (T.sri[:], T.src[:]))
    dma("s", "lth", "", "thi", (T.thi[:], T.th[:]))
    op("g", "", "pi", lambda: g.iota(T.pi[:], [[0, 1]], 0, 1))
    op("g", "", "J", lambda: g.iota(T.J[:], [[1, 144]], -15, 0, allow_small_or_imprecise_dtypes=True))
    op("g", "", "GB", lambda: g.iota(T.GB[:], [[16, 8], [0, 16]], 0, 0, allow_small_or_imprecise_dtypes=True))
    op("g", "", "val", lambda: g.iota(T.val[:], [[1, 48], [KC, 16]], 32, 0, allow_small_or_imprecise_dtypes=True))
    op("v", "", "SWa SWb", lambda: V.memset(T.SW[:], 0.0))
    ts("pi", "gbi", T.gbi[:], T.pi[:], 112, A.bitwise_and)
    cp("pi", "pf", T.pf[:], T.pi[:])
    cp("gbi", "gbf", T.gbf[:], T.gbi[:])
    ts("J gbf", "E", T.E[:], T.J[:], T.gbf[:], A.is_equal)
    ts("pf gbf", "w1", T.w1[:], T.pf[:], T.gbf[:], A.is_equal, BIG - 1.0, A.mult)
    ts("GB gbf", "OB", T.OB[:], T.GB[:], T.gbf[:], A.is_equal)
    ts("GB gbf", "nOB", T.nOB[:], T.GB[:], T.gbf[:], A.is_equal, -1.0, A.mult)
    ts("w1", "w2", T.w2[:], T.w1[:], 1.0, A.add)
    ts("J gbf w2", "E2", T.E2[:], T.J[:], T.gbf[:], A.is_equal, T.w2[:], A.mult)
    ts("tgi", "ci", T.ci[:], T.tgi[:], 8, A.logical_shift_right)
    ts("tgi", "f1", T.f1[:], T.tgi[:], 13.0, A.mult)
    ts("ci", "f2", T.f2[:], T.ci[:], -3327.0, A.mult)
    cp("tgi", "ES0", T.ES0[:], T.tgi[:])
    tt("f1 f2", "f3", T.f3[:], T.f1[:], T.f2[:], A.add)
    cp("f3", "tpu", T.tpu[:], T.f3[:])
    cp("val tpu", "wA", T.wA[:, 0:W].indirect(T.tpu[:, 0:48]), T.val[:])
    op("s", "val tpu", "wB", lambda: S.activation(T.wB[:, 0:W].indirect(T.tpu[:, 48:96]), T.val[:], F.Silu))
    dma("y", "oA", "wA", "uA", (T.uA[:], T.wA[0::16, :]))
    dma("y", "oB", "wB", "uB", (T.uB[:], T.wB[0::16, :]))
    sel("OB", "I", T.I[:], T.OB[:], own, A.is_equal, 0.0, 0)
    sel("nOB", "nJ", T.nJ[:], T.nOB[:], own, A.is_equal, 0.0, 0)
    send("E", 0, 0, "ES0", T.ES0[:])
    sel("nOB", "Ua", T.Ua[:], T.nOB[:], own, A.is_gt, 0.0, 0)
    sel("Ua", "U", T.U[:], T.Ua[:], own, A.not_equal, -2048.0, 0)
    sel("OB", "Sw", T.Sw[:], T.OB[:], mate, A.is_equal, 0.0, -1)
    sel("nOB", "Ub", T.Ub[:], T.nOB[:], mate, A.is_gt, 0.0, -1)
    sel("Ub", "Um", T.Um[:], T.Ub[:], mate, A.not_equal, -2048.0, -1)
    cp("tri", "tru", T.tru[:], T.tri[:])
    cp("sri", "sru", T.sru[:], T.sri[:])
    cp("sri", "srf", T.srf[:], T.sri[:])
    cp("sri", "hi0", T.BS0[:, 0:KC], T.sri[:])
    cp("thi", "thf", T.thf[:], T.thi[:])
    tt("srf hi0", "lo0", T.BS0[:, KC:2 * KC], T.srf[:], T.BS0[:, 0:KC], A.subtract)
    cp("tgi", "tgf", T.tgf[:], T.tgi[:])
    send("B", 0, 0, "hi0 lo0", T.BS0[:])

    def amend_trigger(r):
        ts("", "pH hit", T.hit[:], T.pH[:, 0:KC], BIG, A.is_ge)
        tt("hit d1", "f1", T.f1[:], T.hit[:], T.d1[:], A.mult)
        tt("f1", "trf", T.trf[:], T.f1[:], T.trf[:], A.add)
        if r < RO:
            cp("trf", "tru", T.tru[:], T.trf[:])
        par = [(T.I[:], T.hit[:]), (T.Sw[:], T.hit[:])] + ([(T.I[:], T.pb[:])] if r > 1 else [])
        mm("I Sw hit pb", "pM", T.pM[:, 0:KC], par)
        mm("If nI srf hit", "pM", T.pM[:, KC:2 * KC], [(T.If[:], T.srf[:]), (T.nI[:], T.hit[:])])
        act("", "pH Af", T.Af[:], T.pH[:, 0:KC], F.Relu, bias=-BIG)
        act("", "pM x1", T.x1[:], T.pM[:, 0:KC], F.Abs, bias=-1.0)
        act("x1", "pb", T.pb[:], T.x1[:], F.Abs, bias=-1.0)

    def amend_target(r):
        tt("pb", "pC f2", T.f2[:], T.pC[:, 0:KC], T.pb[:], A.mult)
        tt("f2", "pC tgf", T.tgf[:], T.pC[:, KC:2 * KC], T.f2[:], A.add)
        if r < RO:
            cp("tgf", "ES%d" % r, T["ES%d" % r][:], T.tgf[:])
            send("E", r, 0, "ES%d" % r, T["ES%d" % r][:])

    def amend_source(r):
        tt("Af", "pM srf", T.srf[:], T.pM[:, KC:2 * KC], T.Af[:], A.max)
        if r < RO:
            cp("srf", "sru", T.sru[:], T.srf[:])
            tt("srf pb", "f3", T.f3[:], T.srf[:], T.pb[:], A.mult)

    def masks(c):
        a, b, q, bank = DCH[c]
        mm("nJ V", bank, T[bank][:, 0:16 * (b - a)], [(T.nJ[:], T.V[:, P + 16 * a:P + 16 * b])], stop=False)

    def watched(c):
        a, b, q, bank = DCH[c]
        out, at = T.B[:, 16 * a:16 * b], places.indirect(T.tru[:, a:b])
        if q == "v":
            cp("V tru", "B%d" % c, out, at)
        else:
            act("V tru", "B%d" % c, out, at, F.Identity)
        mm("I B%d" % c, bank, T[bank][:, 0:16 * (b - a)], [(T.I[:], out)], start=False)

    def distance(c):
        a, b, q, bank = DCH[c]
        act("", "%s D%d" % (bank, c), T.D[:, 16 * a:16 * b], T[bank][:, 0:16 * (b - a)], F.Abs)
        mm("E D%d" % c, "pF", T.pF[:, a:b], [(T.E[:, 15 - i:143 - i], T.D[:, 16 * a + i:16 * b:16]) for i in range(16)])

    def message(r, c):
        a, b = MCH[c]
        out = T["mS%d" % r][:, 16 * a:16 * b]
        ts("V", "K%d" % c, T.K[:, 16 * a:16 * b], T.V[:, P + 16 * a:P + 16 * b], 8.0, A.is_lt, 31.0, A.mult)
        tt("V sru K%d" % c, "m%d_%d" % (r, c), out, places.indirect(T.sru[:, a:b]), T.K[:, 16 * a:16 * b], A.max)
        send("m", r, c, "m%d_%d" % (r, c), out)

    def old(r, c):
        a, b = MCH[c]
        act("V aE%d" % r, "Y%d" % c, T.Y[:, 16 * a:16 * b], places.indirect(T["EL%d" % r][:, a:b]), F.Identity, bias=-8.0, scale=0.5)
        mm("I Y%d" % c, "pT%d" % c, T["pT%d" % c][:], [(T.I[:], T.Y[:, 16 * a:16 * b])], stop=False)

    def merge(r, c):
        a, b = MCH[c]
        mm("I am%d_%d" % (r, c), "pT%d" % c, T["pT%d" % c][:], [(T.I[:], T["mL%d" % r][:, 16 * a:16 * b])], start=False)
        act("", "pT%d T%d" % (c, c), T.Tt[:, 16 * a:16 * b], T["pT%d" % c][:], F.Abs, bias=-15.0)

    for r in range(RO):
        OS, BS, GSn = T["OS%d" % r], T["BS%d" % r], T["GS%d" % r]
        masks(0)
        masks(1)
        if r:
            amend_trigger(r)
        masks(2)
        watched(0)
        watched(1)
        if r:
            amend_target(r)
            amend_source(r)
            mm("If SI srf f3", "pM", T.pM[:, 2 * KC:3 * KC], [(T.If[:], T.srf[:]), (T.SI[:], T.f3[:])])
        watched(2)
        distance(0)
        distance(1)
        distance(2)
        message(r, 0)
        if r:
            cp("", "pM hi%d" % r, BS[:, 0:KC], T.pM[:, 2 * KC:3 * KC])
            tt("hi%d" % r, "pM lo%d" % r, BS[:, KC:2 * KC], T.pM[:, 2 * KC:3 * KC], BS[:, 0:KC], A.subtract)
            send("B", r, 0, "hi%d lo%d" % (r, r), BS[:])
            act("pb", "thr0", T.thr[:, 0:KC], T.pb[:], F.Identity, bias=TH, scale=-8192.0)
            act("pb", "thr1", T.thr[:, KC:2 * KC], T.pb[:], F.Identity, bias=TH - 8192.0, scale=8192.0)
        message(r, 1)
        ts("thf", "pF cb", T.cb[:], T.pF[:, 0:KC], T.thf[:], A.is_lt)
        op("v", "cb", "Pb", lambda: V.tensor_tensor_scan(T.Pb[:], T.cb[:], T.cb[:], 0.0, A.add, A.max))
        mm("OB U cb Pb", "pZ", T.pZ[:, 0:KC], [(T.U[:], T.cb[:]), (T.OB[:], T.Pb[:])])
        if r:
            mm("OB Um cb Pb", "pZ", T.pZ[:, KC:2 * KC], [(T.Um[:], T.cb[:]), (T.OB[:], T.Pb[:])])
        ts("", "pZ f4", T.f4[:], T.pZ[:, 0:KC], TH, A.is_gt, float(W), A.mult)
        tt("f4 tgf", "f5", T.f5[:], T.f4[:], T.tgf[:], A.add)
        cp("f5", "G%d" % r, GSn[:], T.f5[:])
        send("G", r, 0, "G%d" % r, GSn[:])
        if r:
            tt("thr0 thr1", "pZ G2", T.G2[:], T.pZ[:, 0:2 * KC], T.thr[:], A.is_le)
            tt("G2", "go%d" % r, OS[:], T.G2[:, 0:KC], T.G2[:, KC:2 * KC], A.add)
        else:
            ts("", "pZ go0", OS[:], T.pZ[:, 0:KC], TH, A.is_le)
        send("O", r, 0, "go%d" % r, OS[:])
        if r == 0:
            ts("uB", "i1", T.i1[:], T.uB[:, :, 7:13], 48.0, A.add)
            tt("uA i1", "i2", T.i2[:], T.uA[:, :, 7:13], T.i1[:], A.min)
            ts("i2", "i3", T.i3[:], T.i2[:], -32.0, A.add)
            cp("i3", "invS", T.invS[:], T.i3[:])
            send("I", 0, 0, "invS", T.invS[:])
        message(r, 2)
        if r == 0:
            cp("tri", "trf", T.trf[:], T.tri[:])
            cp("I", "If", T.If[:], T.I[:])
            tt("I Sw", "SI", T.SI[:], T.Sw[:], T.I[:], A.subtract)
            ts("I", "nI", T.nI[:], T.I[:], -BIG, A.mult)
        tt("srf trf", "d1", T.d1[:], T.srf[:], T.trf[:], A.subtract)
        OL, BL = T["OL%d" % r], T["BL%d" % r]
        rows = [lambda: dma("y", "fl%d" % r, "aO%d" % r, "SWa", (T.SW[0::16, 0:M], OL[:])),
                lambda: dma("y", "fb%d" % r, "aB%d" % r, "SWb", *[(T.SW[1 + i::16, 0:M], BL[:, i * KC:(i + 1) * KC]) for i in range(2)])]
        for f in (rows if r else rows[::-1]):
            f()
        for c in MORD:
            old(r, c)
        for c in MORD:
            merge(r, c)
        if r == 0:
            mm("SI tgf", "pC", T.pC[:, 0:KC], [(T.SI[:], T.tgf[:])])
            mm("If tgf", "pC", T.pC[:, KC:2 * KC], [(T.If[:], T.tgf[:])])
        for c in MORD:
            a, b = MCH[c]
            tt("Y%d T%d aG%d" % (c, c, r), "V", T.V[:, 0:2 * W].indirect(T["GL%d" % r][:, a:b]),
               T.Y[:, 16 * a:16 * b], T.Tt[:, 16 * a:16 * b], A.add)
        for c, (a, b) in enumerate(SCH):
            act("SWa SWb aI", "S%d" % c, T.GS[:, 16 * a:16 * b], T.SW[:, 0:M + 16].indirect(T.invL[:, a:b]), F.Identity)
            mm("E2 S%d" % c, "pH", T.pH[:, 0:KC],
               [(T.E2[:, 15 - i:143 - i], T.GS[:, KC * i:KC * (i + 1)]) for i in range(a // 6, b // 6)], start=c == 0, stop=c == len(SCH) - 1)

    dma("y", "ox", "V", "", (T.yx[:], places))
    amend_trigger(RO)
    amend_source(RO)
    amend_target(RO)
    dma("s", "ol", "trf srf tgf", "", (T.ytrig[:], T.trf[:]), (T.ysrc[:], T.srf[:]), (T.ytg[:], T.tgf[:]))
    for name, val in total.items():
        if seen["g"].get(name, 0) < val:
            g.wait_ge(T.sem[name], val)
